import numpy as np
import ml_dtypes


def mxq(x, axis, fmt="e4m3"):
    dtype, down = {"e4m3": (ml_dtypes.float8_e4m3fn, 7), "e5m2": (ml_dtypes.float8_e5m2, 14)}[fmt]
    v = np.moveaxis(np.asarray(x, np.float32).astype(ml_dtypes.bfloat16).astype(np.float64), axis, -1)
    blocks = v.reshape(v.shape[:-1] + (-1, 32))
    amax = np.abs(blocks).max(-1, keepdims=True)
    byte = np.maximum(np.where(amax > 0, np.frexp(amax)[1] - 1 + 127, 0) - down, 1)
    scale = np.exp2(byte - 127.0)
    codes = (blocks / scale).astype(np.float32).astype(dtype).astype(np.float64)
    return np.moveaxis((codes * scale).reshape(v.shape), -1, axis)


WIDE = False


def mx_kscale(k):
    if not WIDE:
        return np.ones(k)
    levels = np.array([10, -10, 5, -5, 0])
    if k % 512:
        return np.exp2(np.random.permutation(np.resize(levels, k // 32))).repeat(32)
    a = np.empty((k // 512, 16))
    for p in range(k // 512):
        a[p, :8] = np.random.permutation(np.resize(levels, 8))
        for g in range(8):
            far = levels[np.abs(levels - a[p, g]) >= 10]
            a[p, g + 8] = far[np.random.randint(len(far))]
    return np.exp2(a.ravel()).repeat(32)


def f64(x):
    return np.asarray(x).astype(np.float64)


def striped(idx):
    return np.tile(np.asarray(idx).reshape(-1, 16).T, (8, 1)).astype(np.uint16)


def unstriped(offs):
    return offs[:16].T.reshape(-1).astype(np.int64)


E2M1 = np.array([0.0, 0.5, 1.0, 1.5, 2.0, 3.0, 4.0, 6.0, -0.0, -0.5, -1.0, -1.5, -2.0, -3.0, -4.0, -6.0])


def pack_weight(w, fmt):
    k, n = w.shape
    w = f64(np.asarray(w, np.float32).astype(ml_dtypes.bfloat16)).reshape(k // 32, 32, n)
    amax = np.abs(w).max(1)
    if fmt == "e4m3":
        byte = np.frexp(amax)[1] - 1 + 127 - 7
    else:
        mant, ex = np.frexp(amax / 6.0)
        byte = np.where(mant > 0.5, ex, ex - 1) + 127
    byte = np.clip(np.where(amax > 0, byte, 1), 1, 254)
    scaled = (w * np.exp2(127.0 - byte)[:, None, :]).reshape(k, n).astype(np.float32)
    by_word = np.ascontiguousarray(scaled.reshape(k // 512, 128, 4, n).transpose(0, 1, 3, 2))
    if fmt == "e4m3":
        words = by_word.astype(ml_dtypes.float8_e4m3fn).view(np.uint8)
    else:
        c = by_word.astype(ml_dtypes.float4_e2m1fn).view(np.uint8) & 0xF
        words = (c[..., 0::2] | (c[..., 1::2] << 4)).reshape(k // 512, 128, 2 * n)
    return np.ascontiguousarray(words), np.ascontiguousarray(byte.astype(np.uint8).reshape(k // 512, 16, n))


def unpack_weight(words, scales, fmt):
    g, _, n = scales.shape
    words = np.ascontiguousarray(words).reshape(g, 128, n, -1)
    if fmt == "e4m3":
        vals = words.view(ml_dtypes.float8_e4m3fn).astype(np.float64)
    else:
        nib = np.empty((g, 128, n, 4), np.uint8)
        nib[..., 0::2] = words & 0xF
        nib[..., 1::2] = words >> 4
        vals = E2M1[nib]
    vals = vals * np.repeat(np.exp2(scales.astype(np.float64) - 127.0), 8, axis=1)[..., None]
    return vals.transpose(0, 1, 3, 2).reshape(g * 512, n)


D, T, I, Q, E, U, J, C = 512, 2048, 512, 128, 512, 1024, 512, 1024


def setup_inputs():
    n = np.random.standard_normal
    idx = np.random.permutation(T)[:I]
    idx2 = np.random.randint(0, U, J)
    fd = mx_kscale(D)
    fc = mx_kscale(C)
    keysp = pack_weight(n((D, T)) / fd[:, None], "e4m3")
    dkeyp = pack_weight(n((D, U)) / fd[:, None], "e4m3")
    return {
        "query": (n((D, Q)) * 0.2 / np.sqrt(D) * fd[:, None]).astype(np.float32),
        "keys_words": keysp[0],
        "keys_scales": keysp[1],
        "dkey_words": dkeyp[0],
        "dkey_scales": dkeyp[1],
        "mask": (0.3 * n((Q, J))).astype(np.float32),
        "fac": (np.random.uniform(0.5, 2.0, (1, C)) * fc).astype(np.float32),
        "vals": (n((C, E)) / fc[:, None]).astype(np.float32),
        "offs": striped(idx),
        "offs2": striped(idx2),
    }


def reference(query, keys_words, keys_scales, dkey_words, dkey_scales, mask, fac, vals, offs, offs2):
    idx = unstriped(offs)
    idx2 = unstriped(offs2)
    keysu = unpack_weight(keys_words, keys_scales, "e4m3")
    dkeyu = unpack_weight(dkey_words, dkey_scales, "e4m3")
    queryq = mxq(f64(query), 0, "e4m3")
    keysidxg = keysu[:, idx]
    a = queryq.T @ keysidxg
    dkeyidx2g = dkeyu[:, idx2]
    b = queryq.T @ dkeyidx2g
    bm = b + f64(mask)
    s = np.concatenate([a, bm], axis=1)
    p = np.exp(s - np.max(s, axis=1, keepdims=True))
    w = p * f64(fac) / np.sum(p, axis=1, keepdims=True)
    wt = w.T
    wtq = mxq(wt, 0, "e4m3")
    valsq = mxq(f64(vals), 0, "e4m3")
    o = wtq.T @ valsq
    return o

@@ -1,0 +1,186 @@
+from contextlib import ExitStack
+
+import concourse.mybir as mybir
+from concourse.masks import make_identity
+
+D, T, I, Q, E, U, J, C = 512, 2048, 512, 128, 512, 1024, 512, 1024
+FLOPS = 2 * Q * D * (I + J) + 2 * Q * C * E
+
+F32 = mybir.dt.float32
+BF16 = mybir.dt.bfloat16
+I32 = mybir.dt.int32
+U32 = mybir.dt.uint32
+U16 = mybir.dt.uint16
+U8 = mybir.dt.uint8
+FP8X4 = mybir.dt.float8_e4m3fn_x4
+ALU = mybir.AluOpType
+ACT = mybir.ActivationFunctionType
+AX = mybir.AxisListType
+
+P = 128
+H = 256
+
+
+def tile_attend_treeverify_parents_kernel(tc, query, keys_words, keys_scales, dkey_words, dkey_scales, mask, fac, vals, offs, offs2, out):
+    nc = tc.nc
+    with ExitStack() as ctx:
+        sb = ctx.enter_context(tc.tile_pool(name="sb", bufs=1))
+        ps = ctx.enter_context(tc.psum_pool(name="ps", bufs=1))
+
+        def sbt(name, shape, dtype):
+            return sb.tile(shape, dtype, name=name, align_bytes=64)
+
+        list_a = sb.tile([P, I // 16], U16, name="list_a")
+        list_b = sb.tile([P, J // 16], U16, name="list_b")
+        kw = sbt("kw", [P, T], U32)
+        ks = sbt("ks", [P, T], U8)
+        dw = sbt("dw", [P, U], U32)
+        ds = sbt("ds", [P, U], U8)
+        q_raw = sbt("q_raw", [P, 4, Q], F32)
+        mask_sb = sbt("mask_sb", [P, J], F32)
+        fac_col = sbt("fac_col", [P, 2, 4], F32)
+        v_raw = {}
+        v_il = {}
+        v_codes = {}
+        v_scales = {}
+        pieces = [(0, 0), (1, 0), (0, 1), (1, 1)]
+        for g, h in pieces:
+            v_raw[g, h] = sbt("v_raw%d%d" % (g, h), [P, 4, H], F32)
+            v_il[g, h] = sbt("v_il%d%d" % (g, h), [P, H, 4], BF16)
+            v_codes[g, h] = sbt("v_codes%d%d" % (g, h), [P, H], U32)
+            v_scales[g, h] = sbt("v_scales%d%d" % (g, h), [P, H], U8)
+        ident = sbt("ident", [P, P], F32)
+
+        def load_scales(eng, tile, src):
+            for quad in range(4):
+                eng.dma_start(out=tile[32 * quad : 32 * quad + 4, :].bitcast(I32), in_=src[0, 4 * quad : 4 * quad + 4, :].bitcast(I32))
+
+        def load_words(eng, tile, src):
+            eng.dma_start(out=tile[:].bitcast(I32), in_=src[0].rearrange("p n t -> p (n t)").bitcast(I32))
+
+        def load_vals(eng, g, h):
+            eng.dma_start(out=v_raw[g, h][:], in_=vals[512 * g : 512 * (g + 1), H * h : H * (h + 1)].rearrange("(p j) e -> p j e", j=4))
+
+        def interleave(eng, dst, src):
+            d = dst.rearrange("p (c i) t -> p c t i", i=4)
+            s = src.rearrange("p t (c i) -> p c t i", i=4)
+            if eng == "s":
+                nc.scalar.copy(out=d, in_=s)
+            elif eng == "v":
+                nc.vector.tensor_copy(out=d, in_=s)
+            else:
+                nc.gpsimd.tensor_scalar(out=dst, in0=src.rearrange("p t c -> p c t"), scalar1=1.0, scalar2=0.0, op0=ALU.mult, op1=ALU.add)
+
+        def quantize(codes, scales, il):
+            nc.vector.quantize_mx(out=codes.bitcast(FP8X4), scales=scales, in_=il.rearrange("p w j -> p (w j)"))
+
+        def quant_v(g, h):
+            quantize(v_codes[g, h][:], v_scales[g, h][:], v_il[g, h][:])
+
+        def il_v(eng, g, h, lo=0, hi=H):
+            interleave(eng, v_il[g, h][:, lo:hi, :], v_raw[g, h][:, :, lo:hi])
+
+        nc.vector.memset(ds[:].bitcast(I32), 0)
+        nc.vector.memset(ks[:].bitcast(I32), 0)
+        nc.sync.dma_start(list_b[:], offs2)
+        nc.sync.dma_start(out=q_raw[:], in_=query.rearrange("(p j) q -> p j q", j=4))
+        load_scales(nc.sync, ds, dkey_scales)
+        load_words(nc.sync, dw, dkey_words)
+        nc.sync.dma_start(out=mask_sb[:], in_=mask)
+        nc.sync.dma_start(list_a[:], offs)
+        load_scales(nc.sync, ks, keys_scales)
+        load_words(nc.sync, kw, keys_words)
+        nc.sync.dma_start(out=fac_col[:], in_=fac[0].rearrange("(g p t) -> p g t", g=2, t=4))
+        load_vals(nc.sync, 0, 0)
+        load_vals(nc.sync, 1, 0)
+        load_vals(nc.sync, 0, 1)
+        load_vals(nc.sync, 1, 1)
+        make_identity(nc, ident[:])
+
+        dsg = sbt("dsg", [P, J], U8)
+        dwg = sbt("dwg", [P, J], U32)
+        ksg = sbt("ksg", [P, I], U8)
+        kwg = [sbt("kwg%d" % h, [P, H], U32) for h in range(2)]
+        q_il = sbt("q_il", [P, Q, 4], BF16)
+        q_codes = sbt("q_codes", [P, Q], U32)
+        q_scales = sbt("q_scales", [P, Q], U8)
+        interleave("s", q_il[:], q_raw[:])
+        nc.vector.tensor_copy(dsg[:], ds[:].indirect(list_b[:]))
+        nc.vector.tensor_copy(dwg[:], dw[:].indirect(list_b[:]))
+        quantize(q_codes[:], q_scales[:], q_il[:])
+        nc.vector.tensor_copy(ksg[:], ks[:].indirect(list_a[:]))
+
+        ps_b = ps.tile([P, J], F32, name="ps_b", tag="bank0")
+        nc.tensor.matmul_mx(out=ps_b[:], lhsT=q_codes[:].bitcast(FP8X4), lhsT_scale=q_scales[:], rhs=dwg[:].bitcast(FP8X4), rhs_scale=dsg[:], start=True, stop=True)
+
+        fac_b = [ps.tile([P, 4, P], F32, name="fac_b%d" % g, tag="fac%d" % g) for g in range(2)]
+        for g in (1, 0):
+            for t in range(4):
+                nc.tensor.transpose(fac_b[g][:, t, :], fac_col[:, g, t : t + 1].to_broadcast([P, P]), ident[:])
+
+        il_v("s", 0, 0)
+        bm = sbt("bm", [P, J], F32)
+        nmax_b = sbt("nmax_b", [P, 1], F32)
+        sum_b = sbt("sum_b", [P, 1], F32)
+        p_b = sbt("p_b", [P, 2, P, 2], F32)
+        nc.vector.tensor_tensor(out=bm[:], in0=ps_b[:], in1=mask_sb[:], op=ALU.add)
+        nc.vector.tensor_copy(kwg[0][:], kw[:].indirect(list_a[:, 0:16]))
+        nc.vector.tensor_reduce(out=nmax_b[:], in_=bm[:], axis=AX.X, op=ALU.max, negate=True)
+        nc.vector.tensor_copy(kwg[1][:], kw[:].indirect(list_a[:, 16:32]))
+        nc.scalar.activation(out=p_b[:].rearrange("q u p e -> q p u e"), in_=bm[:].rearrange("q (p u e) -> q p u e", u=2, e=2), func=ACT.Exp, bias=nmax_b[:], scale=1.0, accum_out=sum_b[:])
+
+        neg_a = sbt("neg_a", [P, 2, P, 2], F32)
+        nmax = [sbt("nmax%d" % h, [P, 1], F32) for h in range(2)]
+        for h in range(2):
+            ps_a = ps.tile([P, H], F32, name="ps_a%d" % h, tag="bank%d" % (1 + h))
+            nc.tensor.matmul_mx(out=ps_a[:], lhsT=q_codes[:].bitcast(FP8X4), lhsT_scale=q_scales[:], rhs=kwg[h][:].bitcast(FP8X4), rhs_scale=ksg[:, H * h : H * (h + 1)], start=True, stop=True)
+            nc.vector.tensor_scalar(out=neg_a[:, :, 64 * h : 64 * (h + 1), :], in0=ps_a[:].rearrange("q (p u e) -> q u p e", u=2, e=2), scalar1=-1.0, scalar2=(nmax_b if h == 0 else nmax[0])[:], op0=ALU.mult, op1=ALU.min, accum_out=nmax[h][:])
+
+        corr = sbt("corr", [P, 1], F32)
+        sum_a = sbt("sum_a", [P, 1], F32)
+        p_a = sbt("p_a", [P, 2, 2 * P], F32)
+        nc.scalar.activation(out=corr[:], in_=nmax_b[:], func=ACT.Exp, bias=nmax[1][:], scale=-1.0)
+        nc.scalar.activation(out=p_a[:].rearrange("q u n -> q (u n)"), in_=neg_a[:].rearrange("q u p e -> q (u p e)"), func=ACT.Exp, bias=nmax[1][:], scale=-1.0, accum_out=sum_a[:])
+        il_v("v", 1, 0)
+        pf_b = sbt("pf_b", [P, 2, P, 2], F32)
+        for u in range(2):
+            nc.vector.scalar_tensor_tensor(out=pf_b[:, u, :, :], in0=p_b[:, u, :, :], scalar=corr[:], in1=fac_b[1][:, 2 * u : 2 * u + 2, :].rearrange("q e p -> q p e"), op0=ALU.mult, op1=ALU.mult)
+        total = sbt("total", [P, 1], F32)
+        rinv = sbt("rinv", [P, 1], F32)
+        nc.vector.tensor_scalar(out=total[:], in0=sum_b[:], scalar1=corr[:], scalar2=sum_a[:], op0=ALU.mult, op1=ALU.add)
+        nc.vector.reciprocal(out=rinv[:], in_=total[:])
+        il_v("s", 0, 1, 0, 128)
+
+        w = [[sbt("w%d%d" % (g, u), [P, 2 * P], BF16) for u in range(2)] for g in range(2)]
+        xt = [ps.tile([P, 2, P], F32, name="xt%d" % g, tag="bank%d" % (1 + g)) for g in range(2)]
+        for u in range(2):
+            nc.vector.scalar_tensor_tensor(out=w[0][u][:].rearrange("q (p e) -> q p e", e=2), in0=p_a[:, u, :].rearrange("q (p e) -> q p e", e=2), scalar=rinv[:], in1=fac_b[0][:, 2 * u : 2 * u + 2, :].rearrange("q e p -> q p e"), op0=ALU.mult, op1=ALU.mult)
+            nc.scalar.activation(out=w[1][u][:], in_=pf_b[:, u, :, :].rearrange("q p e -> q (p e)"), func=ACT.Copy, scale=rinv[:])
+            for g in range(2):
+                nc.tensor.transpose(xt[g][:, u, :], w[g][u][:].bitcast(F32), ident[:])
+        quant_v(0, 0)
+        quant_v(1, 0)
+        il_v("s", 0, 1, 128, 256)
+        w_il = [sbt("w_il%d" % g, [P, Q, 4], BF16) for g in range(2)]
+        w_codes = [sbt("w_codes%d" % g, [P, Q], U32) for g in range(2)]
+        w_scales = [sbt("w_scales%d" % g, [P, Q], U8) for g in range(2)]
+        for g in range(2):
+            dst = w_il[g][:].rearrange("p r t -> p (r t)").bitcast(F32).rearrange("p (r u) -> p r u", u=2)
+            src = xt[g][:].rearrange("p u r -> p r u")
+            if g == 0:
+                nc.scalar.copy(out=dst, in_=src)
+            else:
+                nc.vector.tensor_copy(out=dst, in_=src)
+        il_v("s", 1, 1, 0, 128)
+        for g in range(2):
+            quantize(w_codes[g][:], w_scales[g][:], w_il[g][:])
+        il_v("v", 1, 1, 128, 256)
+        quant_v(0, 1)
+        quant_v(1, 1)
+        for h in range(2):
+            acc = ps.tile([P, H], F32, name="acc%d" % h, tag="acc%d" % h)
+            for g in range(2):
+                nc.tensor.matmul_mx(out=acc[:], lhsT=w_codes[g][:].bitcast(FP8X4), lhsT_scale=w_scales[g][:], rhs=v_codes[g, h][:].bitcast(FP8X4), rhs_scale=v_scales[g, h][:], start=(g == 0), stop=(g == 1))
+            res = sbt("res%d" % h, [P, H], F32)
+            nc.scalar.copy(out=res[:], in_=acc[:])
+            nc.sync.dma_start(out=out[:, H * h : H * (h + 1)], in_=res[:])

@@ -25,15 +25,19 @@ def tile_attend_treeverify_parents_kernel(tc, query, keys_words, keys_scales, dk
     nc = tc.nc
     with ExitStack() as ctx:
         sb = ctx.enter_context(tc.tile_pool(name="sb", bufs=1))
+        shared = ctx.enter_context(tc.tile_pool(name="shared", bufs=1))
         ps = ctx.enter_context(tc.psum_pool(name="ps", bufs=1))
 
-        def sbt(name, shape, dtype):
-            return sb.tile(shape, dtype, name=name, align_bytes=64)
+        def sbt(name, shape, dtype, tag=None):
+            return sb.tile(shape, dtype, name=name, tag=tag or name, align_bytes=64)
+
+        def placed(name, shape, dtype, offset):
+            return shared.tile(shape, dtype, name=name, align_bytes=64, offset=offset)
 
         list_a = sb.tile([P, I // 16], U16, name="list_a")
         list_b = sb.tile([P, J // 16], U16, name="list_b")
         kw = sbt("kw", [P, T], U32)
-        ks = sbt("ks", [P, T], U8)
+        ks = placed("ks", [P, T], U8, 512)
         dw = sbt("dw", [P, U], U32)
         ds = sbt("ds", [P, U], U8)
         q_raw = sbt("q_raw", [P, 4, Q], F32)
@@ -46,13 +50,10 @@ def tile_attend_treeverify_parents_kernel(tc, query, keys_words, keys_scales, dk
         pieces = [(0, 0), (1, 0), (0, 1), (1, 1)]
         for g, h in pieces:
             v_raw[g, h] = sbt("v_raw%d%d" % (g, h), [P, 4, H], F32)
-            v_il[g, h] = sbt("v_il%d%d" % (g, h), [P, H, 4], BF16)
-            v_codes[g, h] = sbt("v_codes%d%d" % (g, h), [P, H], U32)
-            v_scales[g, h] = sbt("v_scales%d%d" % (g, h), [P, H], U8)
         ident = sbt("ident", [P, P], F32)
 
-        def load_scales(eng, tile, src):
-            for quad in range(4):
+        def load_scales(eng, tile, src, quads):
+            for quad in quads:
                 eng.dma_start(out=tile[32 * quad : 32 * quad + 4, :].bitcast(I32), in_=src[0, 4 * quad : 4 * quad + 4, :].bitcast(I32))
 
         def load_words(eng, tile, src):
@@ -74,23 +75,29 @@ def tile_attend_treeverify_parents_kernel(tc, query, keys_words, keys_scales, dk
         def quantize(codes, scales, il):
             nc.vector.quantize_mx(out=codes.bitcast(FP8X4), scales=scales, in_=il.rearrange("p w j -> p (w j)"))
 
-        def quant_v(g, h):
-            quantize(v_codes[g, h][:], v_scales[g, h][:], v_il[g, h][:])
+        def quant_v(g, h, lo, hi, offset=None):
+            if (g, h) not in v_codes:
+                v_codes[g, h] = sbt("v_codes%d%d" % (g, h), [P, H], U32)
+                name = "v_scales%d%d" % (g, h)
+                v_scales[g, h] = sbt(name, [P, H], U8) if offset is None else placed(name, [P, H], U8, offset)
+            quantize(v_codes[g, h][:, lo:hi], v_scales[g, h][:, lo:hi], v_il[g, h, lo][:])
 
-        def il_v(eng, g, h, lo=0, hi=H):
-            interleave(eng, v_il[g, h][:, lo:hi, :], v_raw[g, h][:, :, lo:hi])
+        def il_v(eng, g, h, lo, hi, tag):
+            name = "v_il%d%d%d" % (g, h, lo)
+            v_il[g, h, lo] = placed(name, [P, hi - lo, 4], BF16, tag) if isinstance(tag, int) else sbt(name, [P, hi - lo, 4], BF16, tag)
+            interleave(eng, v_il[g, h, lo][:], v_raw[g, h][:, :, lo:hi])
 
         nc.vector.memset(ds[:].bitcast(I32), 0)
         nc.vector.memset(ks[:].bitcast(I32), 0)
         nc.sync.dma_start(list_b[:], offs2)
         nc.sync.dma_start(out=q_raw[:], in_=query.rearrange("(p j) q -> p j q", j=4))
-        load_scales(nc.sync, ds, dkey_scales)
+        load_scales(nc.sync, ds, dkey_scales, (0, 1, 2, 3))
         load_words(nc.sync, dw, dkey_words)
         nc.sync.dma_start(out=mask_sb[:], in_=mask)
         nc.sync.dma_start(list_a[:], offs)
-        load_scales(nc.sync, ks, keys_scales)
+        load_scales(nc.sync, ks, keys_scales, (0, 1, 2, 3))
         load_words(nc.sync, kw, keys_words)
-        nc.sync.dma_start(out=fac_col[:], in_=fac[0].rearrange("(g p t) -> p g t", g=2, t=4))
+        nc.gpsimd.dma_start(out=fac_col[:], in_=fac[0].rearrange("(g p t) -> p g t", g=2, t=4))
         load_vals(nc.sync, 0, 0)
         load_vals(nc.sync, 1, 0)
         load_vals(nc.sync, 0, 1)
@@ -100,7 +107,6 @@ def tile_attend_treeverify_parents_kernel(tc, query, keys_words, keys_scales, dk
         dsg = sbt("dsg", [P, J], U8)
         dwg = sbt("dwg", [P, J], U32)
         ksg = sbt("ksg", [P, I], U8)
-        kwg = [sbt("kwg%d" % h, [P, H], U32) for h in range(2)]
         q_il = sbt("q_il", [P, Q, 4], BF16)
         q_codes = sbt("q_codes", [P, Q], U32)
         q_scales = sbt("q_scales", [P, Q], U8)
@@ -118,69 +124,91 @@ def tile_attend_treeverify_parents_kernel(tc, query, keys_words, keys_scales, dk
             for t in range(4):
                 nc.tensor.transpose(fac_b[g][:, t, :], fac_col[:, g, t : t + 1].to_broadcast([P, P]), ident[:])
 
-        il_v("s", 0, 0)
-        bm = sbt("bm", [P, J], F32)
-        nmax_b = sbt("nmax_b", [P, 1], F32)
+        bm = placed("bm", [P, J], F32, 2048)
+        kwg = [placed("kwg%d" % h, [P, H], U32, 1024 * h) for h in range(2)]
         sum_b = sbt("sum_b", [P, 1], F32)
-        p_b = sbt("p_b", [P, 2, P, 2], F32)
         nc.vector.tensor_tensor(out=bm[:], in0=ps_b[:], in1=mask_sb[:], op=ALU.add)
         nc.vector.tensor_copy(kwg[0][:], kw[:].indirect(list_a[:, 0:16]))
-        nc.vector.tensor_reduce(out=nmax_b[:], in_=bm[:], axis=AX.X, op=ALU.max, negate=True)
         nc.vector.tensor_copy(kwg[1][:], kw[:].indirect(list_a[:, 16:32]))
+        nmax_b = sbt("nmax_b", [P, 1], F32, "kw")
+        nc.vector.tensor_reduce(out=nmax_b[:], in_=bm[:], axis=AX.X, op=ALU.max, negate=True)
+        il_v("s", 0, 0, 0, 256, None)
+        il_v("s", 1, 0, 0, 128, None)
+        p_b = sbt("p_b", [P, 2, P, 2], F32, "v_raw00")
         nc.scalar.activation(out=p_b[:].rearrange("q u p e -> q p u e"), in_=bm[:].rearrange("q (p u e) -> q p u e", u=2, e=2), func=ACT.Exp, bias=nmax_b[:], scale=1.0, accum_out=sum_b[:])
 
-        neg_a = sbt("neg_a", [P, 2, P, 2], F32)
-        nmax = [sbt("nmax%d" % h, [P, 1], F32) for h in range(2)]
-        for h in range(2):
-            ps_a = ps.tile([P, H], F32, name="ps_a%d" % h, tag="bank%d" % (1 + h))
-            nc.tensor.matmul_mx(out=ps_a[:], lhsT=q_codes[:].bitcast(FP8X4), lhsT_scale=q_scales[:], rhs=kwg[h][:].bitcast(FP8X4), rhs_scale=ksg[:, H * h : H * (h + 1)], start=True, stop=True)
-            nc.vector.tensor_scalar(out=neg_a[:, :, 64 * h : 64 * (h + 1), :], in0=ps_a[:].rearrange("q (p u e) -> q u p e", u=2, e=2), scalar1=-1.0, scalar2=(nmax_b if h == 0 else nmax[0])[:], op0=ALU.mult, op1=ALU.min, accum_out=nmax[h][:])
 
-        corr = sbt("corr", [P, 1], F32)
+        neg_a = placed("neg_a", [P, 2, P, 2], F32, 5120)
+        nmax = sbt("nmax", [P, 1], F32)
+        ps_a = ps.tile([P, I], F32, name="ps_a", tag="bank1")
+        for h in range(2):
+            nc.tensor.matmul_mx(out=ps_a[:, H * h : H * (h + 1)], lhsT=q_codes[:].bitcast(FP8X4), lhsT_scale=q_scales[:], rhs=kwg[h][:].bitcast(FP8X4), rhs_scale=ksg[:, H * h : H * (h + 1)], start=True, stop=True)
+
+        nc.vector.tensor_scalar(out=neg_a[:], in0=ps_a[:].rearrange("q (p u e) -> q u p e", u=2, e=2), scalar1=-1.0, scalar2=nmax_b[:], op0=ALU.mult, op1=ALU.min, accum_out=nmax[:])
+
+        corr = placed("corr", [P, 1], F32, 2048)
         sum_a = sbt("sum_a", [P, 1], F32)
-        p_a = sbt("p_a", [P, 2, 2 * P], F32)
-        nc.scalar.activation(out=corr[:], in_=nmax_b[:], func=ACT.Exp, bias=nmax[1][:], scale=-1.0)
-        nc.scalar.activation(out=p_a[:].rearrange("q u n -> q (u n)"), in_=neg_a[:].rearrange("q u p e -> q (u p e)"), func=ACT.Exp, bias=nmax[1][:], scale=-1.0, accum_out=sum_a[:])
-        il_v("v", 1, 0)
-        pf_b = sbt("pf_b", [P, 2, P, 2], F32)
+        p_a = placed("p_a", [P, 2, P, 2], F32, 2112)
+        nc.scalar.activation(out=corr[:], in_=nmax_b[:], func=ACT.Exp, bias=nmax[:], scale=-1.0)
+        nc.scalar.activation(out=p_a[:].rearrange("q u p e -> q (u p e)"), in_=neg_a[:].rearrange("q u p e -> q (u p e)"), func=ACT.Exp, bias=nmax[:], scale=-1.0, accum_out=sum_a[:])
+        quant_v(0, 0, 0, 256, 1024)
+        il_v("s", 1, 0, 128, 256, 4160)
+        il_v("s", 0, 1, 0, 128, 5632)
+        il_v("s", 1, 1, 128, 256, 7104)
+        pf = [placed("pf%d" % g, [P, 2, P, 2], F32, 8192 + 2048 * g) for g in range(2)]
         for u in range(2):
-            nc.vector.scalar_tensor_tensor(out=pf_b[:, u, :, :], in0=p_b[:, u, :, :], scalar=corr[:], in1=fac_b[1][:, 2 * u : 2 * u + 2, :].rearrange("q e p -> q p e"), op0=ALU.mult, op1=ALU.mult)
+            nc.vector.scalar_tensor_tensor(out=pf[1][:, u, :, :], in0=p_b[:, u, :, :], scalar=corr[:], in1=fac_b[1][:, 2 * u : 2 * u + 2, :].rearrange("q e p -> q p e"), op0=ALU.mult, op1=ALU.mult)
         total = sbt("total", [P, 1], F32)
         rinv = sbt("rinv", [P, 1], F32)
+
+        def weigh_a(u):
+            nc.vector.tensor_tensor(out=pf[0][:, u, :, :], in0=fac_b[0][:, 2 * u : 2 * u + 2, :].rearrange("q e p -> q p e"), in1=p_a[:, u, :, :], op=ALU.mult)
+
+        weigh_a(0)
         nc.vector.tensor_scalar(out=total[:], in0=sum_b[:], scalar1=corr[:], scalar2=sum_a[:], op0=ALU.mult, op1=ALU.add)
+        weigh_a(1)
         nc.vector.reciprocal(out=rinv[:], in_=total[:])
-        il_v("s", 0, 1, 0, 128)
+
 
         w = [[sbt("w%d%d" % (g, u), [P, 2 * P], BF16) for u in range(2)] for g in range(2)]
         xt = [ps.tile([P, 2, P], F32, name="xt%d" % g, tag="bank%d" % (1 + g)) for g in range(2)]
-        for u in range(2):
-            nc.vector.scalar_tensor_tensor(out=w[0][u][:].rearrange("q (p e) -> q p e", e=2), in0=p_a[:, u, :].rearrange("q (p e) -> q p e", e=2), scalar=rinv[:], in1=fac_b[0][:, 2 * u : 2 * u + 2, :].rearrange("q e p -> q p e"), op0=ALU.mult, op1=ALU.mult)
-            nc.scalar.activation(out=w[1][u][:], in_=pf_b[:, u, :, :].rearrange("q p e -> q (p e)"), func=ACT.Copy, scale=rinv[:])
-            for g in range(2):
+        for g in range(2):
+            for u in range(2):
+                src = pf[g][:, u, :, :].rearrange("q p e -> q (p e)")
+                if (g, u) in []:
+                    nc.scalar.activation(out=w[g][u][:], in_=src, func=ACT.Copy, scale=rinv[:])
+                else:
+                    nc.vector.tensor_scalar(out=w[g][u][:], in0=src, scalar1=rinv[:], scalar2=None, op0=ALU.mult)
                 nc.tensor.transpose(xt[g][:, u, :], w[g][u][:].bitcast(F32), ident[:])
-        quant_v(0, 0)
-        quant_v(1, 0)
-        il_v("s", 0, 1, 128, 256)
+        il_v("v", 0, 1, 128, 256, 10240)
+        il_v("v", 1, 1, 0, 128, 11264)
+        quant_v(1, 0, 0, 128, 8192)
+        quant_v(1, 0, 128, 256)
         w_il = [sbt("w_il%d" % g, [P, Q, 4], BF16) for g in range(2)]
         w_codes = [sbt("w_codes%d" % g, [P, Q], U32) for g in range(2)]
         w_scales = [sbt("w_scales%d" % g, [P, Q], U8) for g in range(2)]
         for g in range(2):
             dst = w_il[g][:].rearrange("p r t -> p (r t)").bitcast(F32).rearrange("p (r u) -> p r u", u=2)
             src = xt[g][:].rearrange("p u r -> p r u")
-            if g == 0:
+            if g in [0, 1]:
                 nc.scalar.copy(out=dst, in_=src)
             else:
                 nc.vector.tensor_copy(out=dst, in_=src)
-        il_v("s", 1, 1, 0, 128)
-        for g in range(2):
+
+        def quant_w(g):
             quantize(w_codes[g][:], w_scales[g][:], w_il[g][:])
-        il_v("v", 1, 1, 128, 256)
-        quant_v(0, 1)
-        quant_v(1, 1)
-        for h in range(2):
-            acc = ps.tile([P, H], F32, name="acc%d" % h, tag="acc%d" % h)
-            for g in range(2):
-                nc.tensor.matmul_mx(out=acc[:], lhsT=w_codes[g][:].bitcast(FP8X4), lhsT_scale=w_scales[g][:], rhs=v_codes[g, h][:].bitcast(FP8X4), rhs_scale=v_scales[g, h][:], start=(g == 0), stop=(g == 1))
-            res = sbt("res%d" % h, [P, H], F32)
-            nc.scalar.copy(out=res[:], in_=acc[:])
-            nc.sync.dma_start(out=out[:, H * h : H * (h + 1)], in_=res[:])
+
+        quant_w(0)
+        quant_v(0, 1, 0, 128)
+        quant_v(0, 1, 128, 256)
+        quant_w(1)
+        quant_v(1, 1, 0, 128)
+        quant_v(1, 1, 128, 256)
+        acc = [ps.tile([P, H], F32, name="acc%d" % h, tag="acc%d" % h) for h in range(2)]
+        for g, h in [(0, 0), (0, 1), (1, 0), (1, 1)]:
+            nc.tensor.matmul_mx(out=acc[h][:], lhsT=w_codes[g][:].bitcast(FP8X4), lhsT_scale=w_scales[g][:], rhs=v_codes[g, h][:].bitcast(FP8X4), rhs_scale=v_scales[g, h][:], start=(g == 0), stop=(g == 1))
+        res = [sbt("res%d" % h, [P, H], F32) for h in range(2)]
+        nc.scalar.copy(out=res[0][:], in_=acc[0][:])
+        nc.scalar.dma_start(out=out[:, 0:H], in_=res[0][:])
+        nc.vector.tensor_copy(out=res[1][:], in_=acc[1][:])
+        nc.sync.dma_start(out=out[:, H:E], in_=res[1][:])

@@ -97,8 +97,8 @@ def tile_attend_treeverify_parents_kernel(tc, query, keys_words, keys_scales, dk
         nc.sync.dma_start(list_a[:], offs)
         load_scales(nc.sync, ks, keys_scales, (0, 1, 2, 3))
         load_words(nc.sync, kw, keys_words)
-        nc.gpsimd.dma_start(out=fac_col[:], in_=fac[0].rearrange("(g p t) -> p g t", g=2, t=4))
         load_vals(nc.sync, 0, 0)
+        nc.sync.dma_start(out=fac_col[:], in_=fac[0].rearrange("(g p t) -> p g t", g=2, t=4))
         load_vals(nc.sync, 1, 0)
         load_vals(nc.sync, 0, 1)
         load_vals(nc.sync, 1, 1)
@@ -119,11 +119,6 @@ def tile_attend_treeverify_parents_kernel(tc, query, keys_words, keys_scales, dk
         ps_b = ps.tile([P, J], F32, name="ps_b", tag="bank0")
         nc.tensor.matmul_mx(out=ps_b[:], lhsT=q_codes[:].bitcast(FP8X4), lhsT_scale=q_scales[:], rhs=dwg[:].bitcast(FP8X4), rhs_scale=dsg[:], start=True, stop=True)
 
-        fac_b = [ps.tile([P, 4, P], F32, name="fac_b%d" % g, tag="fac%d" % g) for g in range(2)]
-        for g in (1, 0):
-            for t in range(4):
-                nc.tensor.transpose(fac_b[g][:, t, :], fac_col[:, g, t : t + 1].to_broadcast([P, P]), ident[:])
-
         bm = placed("bm", [P, J], F32, 2048)
         kwg = [placed("kwg%d" % h, [P, H], U32, 1024 * h) for h in range(2)]
         sum_b = sbt("sum_b", [P, 1], F32)
@@ -143,6 +138,11 @@ def tile_attend_treeverify_parents_kernel(tc, query, keys_words, keys_scales, dk
         ps_a = ps.tile([P, I], F32, name="ps_a", tag="bank1")
         for h in range(2):
             nc.tensor.matmul_mx(out=ps_a[:, H * h : H * (h + 1)], lhsT=q_codes[:].bitcast(FP8X4), lhsT_scale=q_scales[:], rhs=kwg[h][:].bitcast(FP8X4), rhs_scale=ksg[:, H * h : H * (h + 1)], start=True, stop=True)
+
+        fac_b = [ps.tile([P, 4, P], F32, name="fac_b%d" % g, tag="fac%d" % g) for g in range(2)]
+        for g in (1, 0):
+            for t in range(4):
+                nc.tensor.transpose(fac_b[g][:, t, :], fac_col[:, g, t : t + 1].to_broadcast([P, P]), ident[:])
 
         nc.vector.tensor_scalar(out=neg_a[:], in0=ps_a[:].rearrange("q (p u e) -> q u p e", u=2, e=2), scalar1=-1.0, scalar2=nmax_b[:], op0=ALU.mult, op1=ALU.min, accum_out=nmax[:])
 

@@ -29,7 +29,7 @@ def tile_attend_treeverify_parents_kernel(tc, query, keys_words, keys_scales, dk
         ps = ctx.enter_context(tc.psum_pool(name="ps", bufs=1))
 
         def sbt(name, shape, dtype, tag=None):
-            return sb.tile(shape, dtype, name=name, tag=tag or name, align_bytes=64)
+            return sb.tile(shape, dtype, name=name, tag=tag or name, align_bytes=256)
 
         def placed(name, shape, dtype, offset):
             return shared.tile(shape, dtype, name=name, align_bytes=64, offset=offset)
@@ -128,7 +128,8 @@ def tile_attend_treeverify_parents_kernel(tc, query, keys_words, keys_scales, dk
         nmax_b = sbt("nmax_b", [P, 1], F32, "kw")
         nc.vector.tensor_reduce(out=nmax_b[:], in_=bm[:], axis=AX.X, op=ALU.max, negate=True)
         il_v("s", 0, 0, 0, 256, None)
-        il_v("s", 1, 0, 0, 128, None)
+        il_v("g", 1, 0, 0, 256, None)
+        il_v("g", 0, 1, 0, 128, None)
         p_b = sbt("p_b", [P, 2, P, 2], F32, "v_raw00")
         nc.scalar.activation(out=p_b[:].rearrange("q u p e -> q p u e"), in_=bm[:].rearrange("q (p u e) -> q p u e", u=2, e=2), func=ACT.Exp, bias=nmax_b[:], scale=1.0, accum_out=sum_b[:])
 
@@ -151,10 +152,8 @@ def tile_attend_treeverify_parents_kernel(tc, query, keys_words, keys_scales, dk
         p_a = placed("p_a", [P, 2, P, 2], F32, 2112)
         nc.scalar.activation(out=corr[:], in_=nmax_b[:], func=ACT.Exp, bias=nmax[:], scale=-1.0)
         nc.scalar.activation(out=p_a[:].rearrange("q u p e -> q (u p e)"), in_=neg_a[:].rearrange("q u p e -> q (u p e)"), func=ACT.Exp, bias=nmax[:], scale=-1.0, accum_out=sum_a[:])
-        quant_v(0, 0, 0, 256, 1024)
-        il_v("s", 1, 0, 128, 256, 4160)
-        il_v("s", 0, 1, 0, 128, 5632)
-        il_v("s", 1, 1, 128, 256, 7104)
+        il_v("s", 1, 1, 0, 256, 4160)
+        il_v("s", 0, 1, 128, 256, 7104)
         pf = [placed("pf%d" % g, [P, 2, P, 2], F32, 8192 + 2048 * g) for g in range(2)]
         for u in range(2):
             nc.vector.scalar_tensor_tensor(out=pf[1][:, u, :, :], in0=p_b[:, u, :, :], scalar=corr[:], in1=fac_b[1][:, 2 * u : 2 * u + 2, :].rearrange("q e p -> q p e"), op0=ALU.mult, op1=ALU.mult)
@@ -180,10 +179,10 @@ def tile_attend_treeverify_parents_kernel(tc, query, keys_words, keys_scales, dk
                 else:
                     nc.vector.tensor_scalar(out=w[g][u][:], in0=src, scalar1=rinv[:], scalar2=None, op0=ALU.mult)
                 nc.tensor.transpose(xt[g][:, u, :], w[g][u][:].bitcast(F32), ident[:])
-        il_v("v", 0, 1, 128, 256, 10240)
-        il_v("v", 1, 1, 0, 128, 11264)
-        quant_v(1, 0, 0, 128, 8192)
-        quant_v(1, 0, 128, 256)
+        quant_v(0, 0, 0, 256, 10240)
+        quant_v(0, 1, 0, 128, 10496)
+        quant_v(0, 1, 128, 256)
+        quant_v(1, 0, 0, 256, 10752)
         w_il = [sbt("w_il%d" % g, [P, Q, 4], BF16) for g in range(2)]
         w_codes = [sbt("w_codes%d" % g, [P, Q], U32) for g in range(2)]
         w_scales = [sbt("w_scales%d" % g, [P, Q], U8) for g in range(2)]
@@ -199,11 +198,8 @@ def tile_attend_treeverify_parents_kernel(tc, query, keys_words, keys_scales, dk
             quantize(w_codes[g][:], w_scales[g][:], w_il[g][:])
 
         quant_w(0)
-        quant_v(0, 1, 0, 128)
-        quant_v(0, 1, 128, 256)
+        quant_v(1, 1, 0, 256, 11008)
         quant_w(1)
-        quant_v(1, 1, 0, 128)
-        quant_v(1, 1, 128, 256)
         acc = [ps.tile([P, H], F32, name="acc%d" % h, tag="acc%d" % h) for h in range(2)]
         for g, h in [(0, 0), (0, 1), (1, 0), (1, 1)]:
             nc.tensor.matmul_mx(out=acc[h][:], lhsT=w_codes[g][:].bitcast(FP8X4), lhsT_scale=w_scales[g][:], rhs=v_codes[g, h][:].bitcast(FP8X4), rhs_scale=v_scales[g, h][:], start=(g == 0), stop=(g == 1))

@@ -18,193 +18,270 @@ ACT = mybir.ActivationFunctionType
 AX = mybir.AxisListType
 
 P = 128
-H = 256
+PACK = 4
+K_PASS = P * PACK
+HALF = 256
+QUARTER = 128
+LIST_ROWS = 16
+PREFIX, DRAFT = 0, 1
+
+KEY_SCALES_AT = 512
+KEY_HALVES_AT = 0
+DRAFT_SCORES_AT = 2048
+CORR_AT = DRAFT_SCORES_AT
+PREFIX_EXP_AT = DRAFT_SCORES_AT + 64
+PREFIX_SCORES_AT = 5120
+WEIGHTED_AT = 8192
+THIRD_QUARTER_AT = PREFIX_SCORES_AT + 64 - 1024
+LAST_QUARTER_AT = WEIGHTED_AT + 2048
+VALUE_SCALES_AT = WEIGHTED_AT
 
 
-def tile_attend_treeverify_parents_kernel(tc, query, keys_words, keys_scales, dkey_words, dkey_scales, mask, fac, vals, offs, offs2, out):
+def tile_attend_treeverify_parents_kernel(
+    tc, query, keys_words, keys_scales, dkey_words, dkey_scales, mask, fac, vals, offs, offs2, out
+):
     nc = tc.nc
     with ExitStack() as ctx:
         sb = ctx.enter_context(tc.tile_pool(name="sb", bufs=1))
         shared = ctx.enter_context(tc.tile_pool(name="shared", bufs=1))
         ps = ctx.enter_context(tc.psum_pool(name="ps", bufs=1))
 
-        def sbt(name, shape, dtype, tag=None):
-            return sb.tile(shape, dtype, name=name, tag=tag or name, align_bytes=256)
+        def new_tile(name, shape, dtype, reuses=None):
+            return sb.tile(shape, dtype, name=name, tag=reuses or name, align_bytes=256)
 
         def placed(name, shape, dtype, offset):
             return shared.tile(shape, dtype, name=name, align_bytes=64, offset=offset)
 
-        list_a = sb.tile([P, I // 16], U16, name="list_a")
-        list_b = sb.tile([P, J // 16], U16, name="list_b")
-        kw = sbt("kw", [P, T], U32)
-        ks = placed("ks", [P, T], U8, 512)
-        dw = sbt("dw", [P, U], U32)
-        ds = sbt("ds", [P, U], U8)
-        q_raw = sbt("q_raw", [P, 4, Q], F32)
-        mask_sb = sbt("mask_sb", [P, J], F32)
-        fac_col = sbt("fac_col", [P, 2, 4], F32)
-        v_raw = {}
-        v_il = {}
-        v_codes = {}
-        v_scales = {}
-        pieces = [(0, 0), (1, 0), (0, 1), (1, 1)]
-        for g, h in pieces:
-            v_raw[g, h] = sbt("v_raw%d%d" % (g, h), [P, 4, H], F32)
-        ident = sbt("ident", [P, P], F32)
+        def load_scales(tile, src):
+            for n in range(4):
+                nc.sync.dma_start(
+                    out=tile[32 * n : 32 * n + 4, :].bitcast(I32), in_=src[0, 4 * n : 4 * n + 4, :].bitcast(I32)
+                )
 
-        def load_scales(eng, tile, src, quads):
-            for quad in quads:
-                eng.dma_start(out=tile[32 * quad : 32 * quad + 4, :].bitcast(I32), in_=src[0, 4 * quad : 4 * quad + 4, :].bitcast(I32))
+        def load_words(tile, src):
+            nc.sync.dma_start(out=tile[:].bitcast(I32), in_=src[0].rearrange("p n t -> p (n t)").bitcast(I32))
 
-        def load_words(eng, tile, src):
-            eng.dma_start(out=tile[:].bitcast(I32), in_=src[0].rearrange("p n t -> p (n t)").bitcast(I32))
+        def load_values(g, h):
+            rows = vals[K_PASS * g : K_PASS * (g + 1), HALF * h : HALF * (h + 1)]
+            nc.sync.dma_start(out=v_raw[g, h][:], in_=rows.rearrange("(p t) e -> p t e", t=PACK))
 
-        def load_vals(eng, g, h):
-            eng.dma_start(out=v_raw[g, h][:], in_=vals[512 * g : 512 * (g + 1), H * h : H * (h + 1)].rearrange("(p j) e -> p j e", j=4))
+        def interleave_on_scalar(dst, src):
+            nc.scalar.copy(
+                out=dst.rearrange("p (c i) t -> p c t i", i=4), in_=src.rearrange("p t (c i) -> p c t i", i=4)
+            )
 
-        def interleave(eng, dst, src):
-            d = dst.rearrange("p (c i) t -> p c t i", i=4)
-            s = src.rearrange("p t (c i) -> p c t i", i=4)
-            if eng == "s":
-                nc.scalar.copy(out=d, in_=s)
-            elif eng == "v":
-                nc.vector.tensor_copy(out=d, in_=s)
-            else:
-                nc.gpsimd.tensor_scalar(out=dst, in0=src.rearrange("p t c -> p c t"), scalar1=1.0, scalar2=0.0, op0=ALU.mult, op1=ALU.add)
+        def interleave_on_gpsimd(dst, src):
+            nc.gpsimd.tensor_scalar(
+                out=dst, in0=src.rearrange("p t c -> p c t"), scalar1=1.0, scalar2=0.0, op0=ALU.mult, op1=ALU.add
+            )
 
-        def quantize(codes, scales, il):
-            nc.vector.quantize_mx(out=codes.bitcast(FP8X4), scales=scales, in_=il.rearrange("p w j -> p (w j)"))
+        def quantize(codes, scales, interleaved):
+            nc.vector.quantize_mx(
+                out=codes.bitcast(FP8X4), scales=scales, in_=interleaved.rearrange("p c t -> p (c t)")
+            )
 
-        def quant_v(g, h, lo, hi, offset=None):
-            if (g, h) not in v_codes:
-                v_codes[g, h] = sbt("v_codes%d%d" % (g, h), [P, H], U32)
-                name = "v_scales%d%d" % (g, h)
-                v_scales[g, h] = sbt(name, [P, H], U8) if offset is None else placed(name, [P, H], U8, offset)
-            quantize(v_codes[g, h][:, lo:hi], v_scales[g, h][:, lo:hi], v_il[g, h, lo][:])
+        def mx_pass(acc, lhs_codes, lhs_scales, rhs_codes, rhs_scales, start, stop):
+            nc.tensor.matmul_mx(
+                out=acc,
+                lhsT=lhs_codes.bitcast(FP8X4),
+                lhsT_scale=lhs_scales,
+                rhs=rhs_codes.bitcast(FP8X4),
+                rhs_scale=rhs_scales,
+                start=start,
+                stop=stop,
+            )
 
-        def il_v(eng, g, h, lo, hi, tag):
-            name = "v_il%d%d%d" % (g, h, lo)
-            v_il[g, h, lo] = placed(name, [P, hi - lo, 4], BF16, tag) if isinstance(tag, int) else sbt(name, [P, hi - lo, 4], BF16, tag)
-            interleave(eng, v_il[g, h, lo][:], v_raw[g, h][:, :, lo:hi])
+        prefix_list = sb.tile([P, I // LIST_ROWS], U16, name="prefix_list")
+        draft_list = sb.tile([P, J // LIST_ROWS], U16, name="draft_list")
+        key_words = new_tile("key_words", [P, T], U32)
+        key_scales = placed("key_scales", [P, T], U8, KEY_SCALES_AT)
+        draft_words = new_tile("draft_words", [P, U], U32)
+        draft_scales = new_tile("draft_scales", [P, U], U8)
+        q_raw = new_tile("q_raw", [P, PACK, Q], F32)
+        mask_sb = new_tile("mask_sb", [P, J], F32)
+        fac_col = new_tile("fac_col", [P, 2, PACK], F32)
+        v_raw = {(g, h): new_tile("v_raw%d%d" % (g, h), [P, PACK, HALF], F32) for h in range(2) for g in range(2)}
+        ident = new_tile("ident", [P, P], F32)
 
-        nc.vector.memset(ds[:].bitcast(I32), 0)
-        nc.vector.memset(ks[:].bitcast(I32), 0)
-        nc.sync.dma_start(list_b[:], offs2)
-        nc.sync.dma_start(out=q_raw[:], in_=query.rearrange("(p j) q -> p j q", j=4))
-        load_scales(nc.sync, ds, dkey_scales, (0, 1, 2, 3))
-        load_words(nc.sync, dw, dkey_words)
+        nc.vector.memset(draft_scales[:].bitcast(I32), 0)
+        nc.vector.memset(key_scales[:].bitcast(I32), 0)
+
+        nc.sync.dma_start(draft_list[:], offs2)
+        nc.sync.dma_start(out=q_raw[:], in_=query.rearrange("(p t) q -> p t q", t=PACK))
+        load_scales(draft_scales, dkey_scales)
+        load_words(draft_words, dkey_words)
         nc.sync.dma_start(out=mask_sb[:], in_=mask)
-        nc.sync.dma_start(list_a[:], offs)
-        load_scales(nc.sync, ks, keys_scales, (0, 1, 2, 3))
-        load_words(nc.sync, kw, keys_words)
-        load_vals(nc.sync, 0, 0)
-        nc.sync.dma_start(out=fac_col[:], in_=fac[0].rearrange("(g p t) -> p g t", g=2, t=4))
-        load_vals(nc.sync, 1, 0)
-        load_vals(nc.sync, 0, 1)
-        load_vals(nc.sync, 1, 1)
+        nc.sync.dma_start(prefix_list[:], offs)
+        load_scales(key_scales, keys_scales)
+        load_words(key_words, keys_words)
+        load_values(PREFIX, 0)
+        nc.sync.dma_start(out=fac_col[:], in_=fac[0].rearrange("(g p t) -> p g t", g=2, t=PACK))
+        load_values(DRAFT, 0)
+        load_values(PREFIX, 1)
+        load_values(DRAFT, 1)
         make_identity(nc, ident[:])
 
-        dsg = sbt("dsg", [P, J], U8)
-        dwg = sbt("dwg", [P, J], U32)
-        ksg = sbt("ksg", [P, I], U8)
-        q_il = sbt("q_il", [P, Q, 4], BF16)
-        q_codes = sbt("q_codes", [P, Q], U32)
-        q_scales = sbt("q_scales", [P, Q], U8)
-        interleave("s", q_il[:], q_raw[:])
-        nc.vector.tensor_copy(dsg[:], ds[:].indirect(list_b[:]))
-        nc.vector.tensor_copy(dwg[:], dw[:].indirect(list_b[:]))
+        draft_scales_g = new_tile("draft_scales_g", [P, J], U8)
+        draft_words_g = new_tile("draft_words_g", [P, J], U32)
+        key_scales_g = new_tile("key_scales_g", [P, I], U8)
+        q_il = new_tile("q_il", [P, Q, PACK], BF16)
+        q_codes = new_tile("q_codes", [P, Q], U32)
+        q_scales = new_tile("q_scales", [P, Q], U8)
+        interleave_on_scalar(q_il[:], q_raw[:])
+        nc.vector.tensor_copy(draft_scales_g[:], draft_scales[:].indirect(draft_list[:]))
+        nc.vector.tensor_copy(draft_words_g[:], draft_words[:].indirect(draft_list[:]))
         quantize(q_codes[:], q_scales[:], q_il[:])
-        nc.vector.tensor_copy(ksg[:], ks[:].indirect(list_a[:]))
+        nc.vector.tensor_copy(key_scales_g[:], key_scales[:].indirect(prefix_list[:]))
+        b_ps = ps.tile([P, J], F32, name="b_ps", tag="bank0")
+        mx_pass(b_ps[:], q_codes[:], q_scales[:], draft_words_g[:], draft_scales_g[:], True, True)
 
-        ps_b = ps.tile([P, J], F32, name="ps_b", tag="bank0")
-        nc.tensor.matmul_mx(out=ps_b[:], lhsT=q_codes[:].bitcast(FP8X4), lhsT_scale=q_scales[:], rhs=dwg[:].bitcast(FP8X4), rhs_scale=dsg[:], start=True, stop=True)
-
-        bm = placed("bm", [P, J], F32, 2048)
-        kwg = [placed("kwg%d" % h, [P, H], U32, 1024 * h) for h in range(2)]
-        sum_b = sbt("sum_b", [P, 1], F32)
-        nc.vector.tensor_tensor(out=bm[:], in0=ps_b[:], in1=mask_sb[:], op=ALU.add)
-        nc.vector.tensor_copy(kwg[0][:], kw[:].indirect(list_a[:, 0:16]))
-        nc.vector.tensor_copy(kwg[1][:], kw[:].indirect(list_a[:, 16:32]))
-        nmax_b = sbt("nmax_b", [P, 1], F32, "kw")
-        nc.vector.tensor_reduce(out=nmax_b[:], in_=bm[:], axis=AX.X, op=ALU.max, negate=True)
-        il_v("s", 0, 0, 0, 256, None)
-        il_v("g", 1, 0, 0, 256, None)
-        il_v("g", 0, 1, 0, 128, None)
-        p_b = sbt("p_b", [P, 2, P, 2], F32, "v_raw00")
-        nc.scalar.activation(out=p_b[:].rearrange("q u p e -> q p u e"), in_=bm[:].rearrange("q (p u e) -> q p u e", u=2, e=2), func=ACT.Exp, bias=nmax_b[:], scale=1.0, accum_out=sum_b[:])
-
-
-        neg_a = placed("neg_a", [P, 2, P, 2], F32, 5120)
-        nmax = sbt("nmax", [P, 1], F32)
-        ps_a = ps.tile([P, I], F32, name="ps_a", tag="bank1")
+        bm = placed("bm", [P, J], F32, DRAFT_SCORES_AT)
+        key_words_g = [placed("key_words_g%d" % h, [P, HALF], U32, KEY_HALVES_AT + 4 * HALF * h) for h in range(2)]
+        draft_sum = new_tile("draft_sum", [P, 1], F32)
+        nc.vector.tensor_tensor(out=bm[:], in0=b_ps[:], in1=mask_sb[:], op=ALU.add)
+        list_cols = HALF // LIST_ROWS
         for h in range(2):
-            nc.tensor.matmul_mx(out=ps_a[:, H * h : H * (h + 1)], lhsT=q_codes[:].bitcast(FP8X4), lhsT_scale=q_scales[:], rhs=kwg[h][:].bitcast(FP8X4), rhs_scale=ksg[:, H * h : H * (h + 1)], start=True, stop=True)
+            offsets = prefix_list[:, list_cols * h : list_cols * (h + 1)]
+            nc.vector.tensor_copy(key_words_g[h][:], key_words[:].indirect(offsets))
+        neg_draft_max = new_tile("neg_draft_max", [P, 1], F32, reuses="key_words")
+        nc.vector.tensor_reduce(out=neg_draft_max[:], in_=bm[:], axis=AX.X, op=ALU.max, negate=True)
 
-        fac_b = [ps.tile([P, 4, P], F32, name="fac_b%d" % g, tag="fac%d" % g) for g in range(2)]
-        for g in (1, 0):
-            for t in range(4):
-                nc.tensor.transpose(fac_b[g][:, t, :], fac_col[:, g, t : t + 1].to_broadcast([P, P]), ident[:])
+        v_il = {}
+        for g, h, interleave in (
+            (PREFIX, 0, interleave_on_scalar),
+            (DRAFT, 0, interleave_on_gpsimd),
+            (PREFIX, 1, interleave_on_gpsimd),
+        ):
+            v_il[g, h] = new_tile("v_il%d%d" % (g, h), [P, HALF, PACK], BF16)
+            interleave(v_il[g, h][:], v_raw[g, h][:])
 
-        nc.vector.tensor_scalar(out=neg_a[:], in0=ps_a[:].rearrange("q (p u e) -> q u p e", u=2, e=2), scalar1=-1.0, scalar2=nmax_b[:], op0=ALU.mult, op1=ALU.min, accum_out=nmax[:])
+        draft_exp = new_tile("draft_exp", [P, 2, P, 2], F32, reuses="v_raw00")
+        nc.scalar.activation(
+            out=draft_exp[:].rearrange("q u p e -> q p u e"),
+            in_=bm[:].rearrange("q (p u e) -> q p u e", u=2, e=2),
+            func=ACT.Exp,
+            bias=neg_draft_max[:],
+            scale=1.0,
+            accum_out=draft_sum[:],
+        )
 
-        corr = placed("corr", [P, 1], F32, 2048)
-        sum_a = sbt("sum_a", [P, 1], F32)
-        p_a = placed("p_a", [P, 2, P, 2], F32, 2112)
-        nc.scalar.activation(out=corr[:], in_=nmax_b[:], func=ACT.Exp, bias=nmax[:], scale=-1.0)
-        nc.scalar.activation(out=p_a[:].rearrange("q u p e -> q (u p e)"), in_=neg_a[:].rearrange("q u p e -> q (u p e)"), func=ACT.Exp, bias=nmax[:], scale=-1.0, accum_out=sum_a[:])
-        il_v("s", 1, 1, 0, 256, 4160)
-        il_v("s", 0, 1, 128, 256, 7104)
-        pf = [placed("pf%d" % g, [P, 2, P, 2], F32, 8192 + 2048 * g) for g in range(2)]
+        neg_a = placed("neg_a", [P, 2, P, 2], F32, PREFIX_SCORES_AT)
+        neg_max = new_tile("neg_max", [P, 1], F32)
+        a_ps = ps.tile([P, I], F32, name="a_ps", tag="bank1")
+        for h in range(2):
+            slots = slice(HALF * h, HALF * (h + 1))
+            mx_pass(a_ps[:, slots], q_codes[:], q_scales[:], key_words_g[h][:], key_scales_g[:, slots], True, True)
+
+        fac_rows = [ps.tile([P, PACK, P], F32, name="fac_rows%d" % g, tag="fac%d" % g) for g in range(2)]
+        for g in (DRAFT, PREFIX):
+            for t in range(PACK):
+                nc.tensor.transpose(fac_rows[g][:, t, :], fac_col[:, g, t : t + 1].to_broadcast([P, P]), ident[:])
+
+        def fac_pair(g, u):
+            return fac_rows[g][:, 2 * u : 2 * u + 2, :].rearrange("q e p -> q p e")
+
+        nc.vector.tensor_scalar(
+            out=neg_a[:],
+            in0=a_ps[:].rearrange("q (p u e) -> q u p e", u=2, e=2),
+            scalar1=-1.0,
+            scalar2=neg_draft_max[:],
+            op0=ALU.mult,
+            op1=ALU.min,
+            accum_out=neg_max[:],
+        )
+
+        corr = placed("corr", [P, 1], F32, CORR_AT)
+        prefix_sum = new_tile("prefix_sum", [P, 1], F32)
+        prefix_exp = placed("prefix_exp", [P, 2, P, 2], F32, PREFIX_EXP_AT)
+        nc.scalar.activation(out=corr[:], in_=neg_draft_max[:], func=ACT.Exp, bias=neg_max[:], scale=-1.0)
+        nc.scalar.activation(
+            out=prefix_exp[:].rearrange("q u p e -> q (u p e)"),
+            in_=neg_a[:].rearrange("q u p e -> q (u p e)"),
+            func=ACT.Exp,
+            bias=neg_max[:],
+            scale=-1.0,
+            accum_out=prefix_sum[:],
+        )
+
+        third_quarter = placed("third_quarter", [P, QUARTER, PACK], BF16, THIRD_QUARTER_AT)
+        interleave_on_scalar(third_quarter[:], v_raw[DRAFT, 1][:, :, 0:QUARTER])
+
+        weighted = [placed("weighted%d" % g, [P, 2, P, 2], F32, WEIGHTED_AT + 4 * K_PASS * g) for g in range(2)]
         for u in range(2):
-            nc.vector.scalar_tensor_tensor(out=pf[1][:, u, :, :], in0=p_b[:, u, :, :], scalar=corr[:], in1=fac_b[1][:, 2 * u : 2 * u + 2, :].rearrange("q e p -> q p e"), op0=ALU.mult, op1=ALU.mult)
-        total = sbt("total", [P, 1], F32)
-        rinv = sbt("rinv", [P, 1], F32)
+            nc.vector.scalar_tensor_tensor(
+                out=weighted[DRAFT][:, u, :, :],
+                in0=draft_exp[:, u, :, :],
+                scalar=corr[:],
+                in1=fac_pair(DRAFT, u),
+                op0=ALU.mult,
+                op1=ALU.mult,
+            )
+        total = new_tile("total", [P, 1], F32)
+        inv_total = new_tile("inv_total", [P, 1], F32)
 
-        def weigh_a(u):
-            nc.vector.tensor_tensor(out=pf[0][:, u, :, :], in0=fac_b[0][:, 2 * u : 2 * u + 2, :].rearrange("q e p -> q p e"), in1=p_a[:, u, :, :], op=ALU.mult)
+        def weigh_prefix(u):
+            nc.vector.tensor_tensor(
+                out=weighted[PREFIX][:, u, :, :], in0=fac_pair(PREFIX, u), in1=prefix_exp[:, u, :, :], op=ALU.mult
+            )
 
-        weigh_a(0)
-        nc.vector.tensor_scalar(out=total[:], in0=sum_b[:], scalar1=corr[:], scalar2=sum_a[:], op0=ALU.mult, op1=ALU.add)
-        weigh_a(1)
-        nc.vector.reciprocal(out=rinv[:], in_=total[:])
+        weigh_prefix(0)
+        nc.vector.tensor_scalar(
+            out=total[:], in0=draft_sum[:], scalar1=corr[:], scalar2=prefix_sum[:], op0=ALU.mult, op1=ALU.add
+        )
+        weigh_prefix(1)
+        nc.vector.reciprocal(out=inv_total[:], in_=total[:])
 
+        w = [[new_tile("w%d%d" % (g, u), [P, 2 * P], BF16) for u in range(2)] for g in range(2)]
+        wt_ps = [ps.tile([P, 2, Q], F32, name="wt_ps%d" % g, tag="bank%d" % (1 + g)) for g in range(2)]
+        for u in range(2):
+            nc.vector.tensor_scalar(
+                out=w[PREFIX][u][:],
+                in0=weighted[PREFIX][:, u, :, :].rearrange("q p e -> q (p e)"),
+                scalar1=inv_total[:],
+                scalar2=None,
+                op0=ALU.mult,
+            )
+            nc.tensor.transpose(wt_ps[PREFIX][:, u, :], w[PREFIX][u][:].bitcast(F32), ident[:])
+            nc.scalar.activation(
+                out=w[DRAFT][u][:],
+                in_=weighted[DRAFT][:, u, :, :].rearrange("q p e -> q (p e)"),
+                func=ACT.Copy,
+                scale=inv_total[:],
+            )
+            nc.tensor.transpose(wt_ps[DRAFT][:, u, :], w[DRAFT][u][:].bitcast(F32), ident[:])
 
-        w = [[sbt("w%d%d" % (g, u), [P, 2 * P], BF16) for u in range(2)] for g in range(2)]
-        xt = [ps.tile([P, 2, P], F32, name="xt%d" % g, tag="bank%d" % (1 + g)) for g in range(2)]
+        last_quarter = placed("last_quarter", [P, QUARTER, PACK], BF16, LAST_QUARTER_AT)
+        interleave_on_scalar(last_quarter[:], v_raw[DRAFT, 1][:, :, QUARTER:HALF])
+
+        v_codes = {}
+        v_scales = {}
+        for n, (g, h) in enumerate(v_il):
+            v_codes[g, h] = new_tile("v_codes%d%d" % (g, h), [P, HALF], U32)
+            v_scales[g, h] = placed("v_scales%d%d" % (g, h), [P, HALF], U8, VALUE_SCALES_AT + HALF * n)
+            quantize(v_codes[g, h][:], v_scales[g, h][:], v_il[g, h][:])
+
+        wt_il = [new_tile("wt_il%d" % g, [P, Q, PACK], BF16) for g in range(2)]
+        wt_codes = [new_tile("wt_codes%d" % g, [P, Q], U32) for g in range(2)]
+        wt_scales = [new_tile("wt_scales%d" % g, [P, Q], U8) for g in range(2)]
+        for g, copy in ((PREFIX, nc.scalar.copy), (DRAFT, nc.vector.tensor_copy)):
+            pairs = wt_il[g][:].rearrange("p q t -> p (q t)").bitcast(F32).rearrange("p (q u) -> p q u", u=2)
+            copy(out=pairs, in_=wt_ps[g][:].rearrange("p u q -> p q u"))
         for g in range(2):
-            for u in range(2):
-                src = pf[g][:, u, :, :].rearrange("q p e -> q (p e)")
-                if (g, u) in []:
-                    nc.scalar.activation(out=w[g][u][:], in_=src, func=ACT.Copy, scale=rinv[:])
-                else:
-                    nc.vector.tensor_scalar(out=w[g][u][:], in0=src, scalar1=rinv[:], scalar2=None, op0=ALU.mult)
-                nc.tensor.transpose(xt[g][:, u, :], w[g][u][:].bitcast(F32), ident[:])
-        quant_v(0, 0, 0, 256, 10240)
-        quant_v(0, 1, 0, 128, 10496)
-        quant_v(0, 1, 128, 256)
-        quant_v(1, 0, 0, 256, 10752)
-        w_il = [sbt("w_il%d" % g, [P, Q, 4], BF16) for g in range(2)]
-        w_codes = [sbt("w_codes%d" % g, [P, Q], U32) for g in range(2)]
-        w_scales = [sbt("w_scales%d" % g, [P, Q], U8) for g in range(2)]
+            quantize(wt_codes[g][:], wt_scales[g][:], wt_il[g][:])
+
+        v_codes[DRAFT, 1] = new_tile("v_codes11", [P, HALF], U32)
+        v_scales[DRAFT, 1] = new_tile("v_scales11", [P, HALF], U8, reuses="wt_il0")
+        for n, quarter in enumerate((third_quarter, last_quarter)):
+            cols = slice(QUARTER * n, QUARTER * (n + 1))
+            quantize(v_codes[DRAFT, 1][:, cols], v_scales[DRAFT, 1][:, cols], quarter[:])
+
+        acc = [ps.tile([P, HALF], F32, name="acc%d" % h, tag="acc%d" % h) for h in range(2)]
         for g in range(2):
-            dst = w_il[g][:].rearrange("p r t -> p (r t)").bitcast(F32).rearrange("p (r u) -> p r u", u=2)
-            src = xt[g][:].rearrange("p u r -> p r u")
-            if g in [0, 1]:
-                nc.scalar.copy(out=dst, in_=src)
-            else:
-                nc.vector.tensor_copy(out=dst, in_=src)
-
-        def quant_w(g):
-            quantize(w_codes[g][:], w_scales[g][:], w_il[g][:])
-
-        quant_w(0)
-        quant_v(1, 1, 0, 256, 11008)
-        quant_w(1)
-        acc = [ps.tile([P, H], F32, name="acc%d" % h, tag="acc%d" % h) for h in range(2)]
-        for g, h in [(0, 0), (0, 1), (1, 0), (1, 1)]:
-            nc.tensor.matmul_mx(out=acc[h][:], lhsT=w_codes[g][:].bitcast(FP8X4), lhsT_scale=w_scales[g][:], rhs=v_codes[g, h][:].bitcast(FP8X4), rhs_scale=v_scales[g, h][:], start=(g == 0), stop=(g == 1))
-        res = [sbt("res%d" % h, [P, H], F32) for h in range(2)]
-        nc.scalar.copy(out=res[0][:], in_=acc[0][:])
-        nc.scalar.dma_start(out=out[:, 0:H], in_=res[0][:])
-        nc.vector.tensor_copy(out=res[1][:], in_=acc[1][:])
-        nc.sync.dma_start(out=out[:, H:E], in_=res[1][:])
+            for h in range(2):
+                mx_pass(
+                    acc[h][:], wt_codes[g][:], wt_scales[g][:], v_codes[g, h][:], v_scales[g, h][:], g == 0, g == 1
+                )
+        for h, copy in enumerate((nc.scalar.copy, nc.vector.tensor_copy)):
+            result = new_tile("result%d" % h, [P, HALF], F32)
+            copy(out=result[:], in_=acc[h][:])
+            nc.sync.dma_start(out=out[:, HALF * h : HALF * (h + 1)], in_=result[:])

from contextlib import ExitStack

import concourse.mybir as mybir
from concourse.masks import make_identity

D, T, I, Q, E, U, J, C = 512, 2048, 512, 128, 512, 1024, 512, 1024
FLOPS = 2 * Q * D * (I + J) + 2 * Q * C * E

F32 = mybir.dt.float32
BF16 = mybir.dt.bfloat16
I32 = mybir.dt.int32
U32 = mybir.dt.uint32
U16 = mybir.dt.uint16
U8 = mybir.dt.uint8
FP8X4 = mybir.dt.float8_e4m3fn_x4
ALU = mybir.AluOpType
ACT = mybir.ActivationFunctionType
AX = mybir.AxisListType

P = 128
PACK = 4
K_PASS = P * PACK
HALF = 256
QUARTER = 128
LIST_ROWS = 16
PREFIX, DRAFT = 0, 1

KEY_SCALES_AT = 512
KEY_HALVES_AT = 0
DRAFT_SCORES_AT = 2048
CORR_AT = DRAFT_SCORES_AT
PREFIX_EXP_AT = DRAFT_SCORES_AT + 64
PREFIX_SCORES_AT = 5120
WEIGHTED_AT = 8192
THIRD_QUARTER_AT = PREFIX_SCORES_AT + 64 - 1024
LAST_QUARTER_AT = WEIGHTED_AT + 2048
VALUE_SCALES_AT = WEIGHTED_AT


def tile_attend_treeverify_parents_kernel(
    tc, query, keys_words, keys_scales, dkey_words, dkey_scales, mask, fac, vals, offs, offs2, out
):
    nc = tc.nc
    with ExitStack() as ctx:
        sb = ctx.enter_context(tc.tile_pool(name="sb", bufs=1))
        shared = ctx.enter_context(tc.tile_pool(name="shared", bufs=1))
        ps = ctx.enter_context(tc.psum_pool(name="ps", bufs=1))

        def new_tile(name, shape, dtype, reuses=None):
            return sb.tile(shape, dtype, name=name, tag=reuses or name, align_bytes=256)

        def placed(name, shape, dtype, offset):
            return shared.tile(shape, dtype, name=name, align_bytes=64, offset=offset)

        def load_scales(tile, src):
            for n in range(4):
                nc.sync.dma_start(
                    out=tile[32 * n : 32 * n + 4, :].bitcast(I32), in_=src[0, 4 * n : 4 * n + 4, :].bitcast(I32)
                )

        def load_words(tile, src):
            nc.sync.dma_start(out=tile[:].bitcast(I32), in_=src[0].rearrange("p n t -> p (n t)").bitcast(I32))

        def load_values(g, h):
            rows = vals[K_PASS * g : K_PASS * (g + 1), HALF * h : HALF * (h + 1)]
            nc.sync.dma_start(out=v_raw[g, h][:], in_=rows.rearrange("(p t) e -> p t e", t=PACK))

        def interleave_on_scalar(dst, src):
            nc.scalar.copy(
                out=dst.rearrange("p (c i) t -> p c t i", i=4), in_=src.rearrange("p t (c i) -> p c t i", i=4)
            )

        def interleave_on_gpsimd(dst, src):
            nc.gpsimd.tensor_scalar(
                out=dst, in0=src.rearrange("p t c -> p c t"), scalar1=1.0, scalar2=0.0, op0=ALU.mult, op1=ALU.add
            )

        def quantize(codes, scales, interleaved):
            nc.vector.quantize_mx(
                out=codes.bitcast(FP8X4), scales=scales, in_=interleaved.rearrange("p c t -> p (c t)")
            )

        def mx_pass(acc, lhs_codes, lhs_scales, rhs_codes, rhs_scales, start, stop):
            nc.tensor.matmul_mx(
                out=acc,
                lhsT=lhs_codes.bitcast(FP8X4),
                lhsT_scale=lhs_scales,
                rhs=rhs_codes.bitcast(FP8X4),
                rhs_scale=rhs_scales,
                start=start,
                stop=stop,
            )

        prefix_list = sb.tile([P, I // LIST_ROWS], U16, name="prefix_list")
        draft_list = sb.tile([P, J // LIST_ROWS], U16, name="draft_list")
        key_words = new_tile("key_words", [P, T], U32)
        key_scales = placed("key_scales", [P, T], U8, KEY_SCALES_AT)
        draft_words = new_tile("draft_words", [P, U], U32)
        draft_scales = new_tile("draft_scales", [P, U], U8)
        q_raw = new_tile("q_raw", [P, PACK, Q], F32)
        mask_sb = new_tile("mask_sb", [P, J], F32)
        fac_col = new_tile("fac_col", [P, 2, PACK], F32)
        v_raw = {(g, h): new_tile("v_raw%d%d" % (g, h), [P, PACK, HALF], F32) for h in range(2) for g in range(2)}
        ident = new_tile("ident", [P, P], F32)

        nc.vector.memset(draft_scales[:].bitcast(I32), 0)
        nc.vector.memset(key_scales[:].bitcast(I32), 0)

        nc.sync.dma_start(draft_list[:], offs2)
        nc.sync.dma_start(out=q_raw[:], in_=query.rearrange("(p t) q -> p t q", t=PACK))
        load_scales(draft_scales, dkey_scales)
        load_words(draft_words, dkey_words)
        nc.sync.dma_start(out=mask_sb[:], in_=mask)
        nc.sync.dma_start(prefix_list[:], offs)
        load_scales(key_scales, keys_scales)
        load_words(key_words, keys_words)
        load_values(PREFIX, 0)
        nc.sync.dma_start(out=fac_col[:], in_=fac[0].rearrange("(g p t) -> p g t", g=2, t=PACK))
        load_values(DRAFT, 0)
        load_values(PREFIX, 1)
        load_values(DRAFT, 1)
        make_identity(nc, ident[:])

        draft_scales_g = new_tile("draft_scales_g", [P, J], U8)
        draft_words_g = new_tile("draft_words_g", [P, J], U32)
        key_scales_g = new_tile("key_scales_g", [P, I], U8)
        q_il = new_tile("q_il", [P, Q, PACK], BF16)
        q_codes = new_tile("q_codes", [P, Q], U32)
        q_scales = new_tile("q_scales", [P, Q], U8)
        interleave_on_scalar(q_il[:], q_raw[:])
        nc.vector.tensor_copy(draft_scales_g[:], draft_scales[:].indirect(draft_list[:]))
        nc.vector.tensor_copy(draft_words_g[:], draft_words[:].indirect(draft_list[:]))
        quantize(q_codes[:], q_scales[:], q_il[:])
        nc.vector.tensor_copy(key_scales_g[:], key_scales[:].indirect(prefix_list[:]))
        b_ps = ps.tile([P, J], F32, name="b_ps", tag="bank0")
        mx_pass(b_ps[:], q_codes[:], q_scales[:], draft_words_g[:], draft_scales_g[:], True, True)

        bm = placed("bm", [P, J], F32, DRAFT_SCORES_AT)
        key_words_g = [placed("key_words_g%d" % h, [P, HALF], U32, KEY_HALVES_AT + 4 * HALF * h) for h in range(2)]
        draft_sum = new_tile("draft_sum", [P, 1], F32)
        nc.vector.tensor_tensor(out=bm[:], in0=b_ps[:], in1=mask_sb[:], op=ALU.add)
        list_cols = HALF // LIST_ROWS
        for h in range(2):
            offsets = prefix_list[:, list_cols * h : list_cols * (h + 1)]
            nc.vector.tensor_copy(key_words_g[h][:], key_words[:].indirect(offsets))
        neg_draft_max = new_tile("neg_draft_max", [P, 1], F32, reuses="key_words")
        nc.vector.tensor_reduce(out=neg_draft_max[:], in_=bm[:], axis=AX.X, op=ALU.max, negate=True)

        v_il = {}
        for g, h, interleave in (
            (PREFIX, 0, interleave_on_scalar),
            (DRAFT, 0, interleave_on_gpsimd),
            (PREFIX, 1, interleave_on_gpsimd),
        ):
            v_il[g, h] = new_tile("v_il%d%d" % (g, h), [P, HALF, PACK], BF16)
            interleave(v_il[g, h][:], v_raw[g, h][:])

        draft_exp = new_tile("draft_exp", [P, 2, P, 2], F32, reuses="v_raw00")
        nc.scalar.activation(
            out=draft_exp[:].rearrange("q u p e -> q p u e"),
            in_=bm[:].rearrange("q (p u e) -> q p u e", u=2, e=2),
            func=ACT.Exp,
            bias=neg_draft_max[:],
            scale=1.0,
            accum_out=draft_sum[:],
        )

        neg_a = placed("neg_a", [P, 2, P, 2], F32, PREFIX_SCORES_AT)
        neg_max = new_tile("neg_max", [P, 1], F32)
        a_ps = ps.tile([P, I], F32, name="a_ps", tag="bank1")
        for h in range(2):
            slots = slice(HALF * h, HALF * (h + 1))
            mx_pass(a_ps[:, slots], q_codes[:], q_scales[:], key_words_g[h][:], key_scales_g[:, slots], True, True)

        fac_rows = [ps.tile([P, PACK, P], F32, name="fac_rows%d" % g, tag="fac%d" % g) for g in range(2)]
        for g in (DRAFT, PREFIX):
            for t in range(PACK):
                nc.tensor.transpose(fac_rows[g][:, t, :], fac_col[:, g, t : t + 1].to_broadcast([P, P]), ident[:])

        def fac_pair(g, u):
            return fac_rows[g][:, 2 * u : 2 * u + 2, :].rearrange("q e p -> q p e")

        nc.vector.tensor_scalar(
            out=neg_a[:],
            in0=a_ps[:].rearrange("q (p u e) -> q u p e", u=2, e=2),
            scalar1=-1.0,
            scalar2=neg_draft_max[:],
            op0=ALU.mult,
            op1=ALU.min,
            accum_out=neg_max[:],
        )

        corr = placed("corr", [P, 1], F32, CORR_AT)
        prefix_sum = new_tile("prefix_sum", [P, 1], F32)
        prefix_exp = placed("prefix_exp", [P, 2, P, 2], F32, PREFIX_EXP_AT)
        nc.scalar.activation(out=corr[:], in_=neg_draft_max[:], func=ACT.Exp, bias=neg_max[:], scale=-1.0)
        nc.scalar.activation(
            out=prefix_exp[:].rearrange("q u p e -> q (u p e)"),
            in_=neg_a[:].rearrange("q u p e -> q (u p e)"),
            func=ACT.Exp,
            bias=neg_max[:],
            scale=-1.0,
            accum_out=prefix_sum[:],
        )

        third_quarter = placed("third_quarter", [P, QUARTER, PACK], BF16, THIRD_QUARTER_AT)
        interleave_on_scalar(third_quarter[:], v_raw[DRAFT, 1][:, :, 0:QUARTER])

        weighted = [placed("weighted%d" % g, [P, 2, P, 2], F32, WEIGHTED_AT + 4 * K_PASS * g) for g in range(2)]
        for u in range(2):
            nc.vector.scalar_tensor_tensor(
                out=weighted[DRAFT][:, u, :, :],
                in0=draft_exp[:, u, :, :],
                scalar=corr[:],
                in1=fac_pair(DRAFT, u),
                op0=ALU.mult,
                op1=ALU.mult,
            )
        total = new_tile("total", [P, 1], F32)
        inv_total = new_tile("inv_total", [P, 1], F32)

        def weigh_prefix(u):
            nc.vector.tensor_tensor(
                out=weighted[PREFIX][:, u, :, :], in0=fac_pair(PREFIX, u), in1=prefix_exp[:, u, :, :], op=ALU.mult
            )

        weigh_prefix(0)
        nc.vector.tensor_scalar(
            out=total[:], in0=draft_sum[:], scalar1=corr[:], scalar2=prefix_sum[:], op0=ALU.mult, op1=ALU.add
        )
        weigh_prefix(1)
        nc.vector.reciprocal(out=inv_total[:], in_=total[:])

        w = [[new_tile("w%d%d" % (g, u), [P, 2 * P], BF16) for u in range(2)] for g in range(2)]
        wt_ps = [ps.tile([P, 2, Q], F32, name="wt_ps%d" % g, tag="bank%d" % (1 + g)) for g in range(2)]
        for u in range(2):
            nc.vector.tensor_scalar(
                out=w[PREFIX][u][:],
                in0=weighted[PREFIX][:, u, :, :].rearrange("q p e -> q (p e)"),
                scalar1=inv_total[:],
                scalar2=None,
                op0=ALU.mult,
            )
            nc.tensor.transpose(wt_ps[PREFIX][:, u, :], w[PREFIX][u][:].bitcast(F32), ident[:])
            nc.scalar.activation(
                out=w[DRAFT][u][:],
                in_=weighted[DRAFT][:, u, :, :].rearrange("q p e -> q (p e)"),
                func=ACT.Copy,
                scale=inv_total[:],
            )
            nc.tensor.transpose(wt_ps[DRAFT][:, u, :], w[DRAFT][u][:].bitcast(F32), ident[:])

        last_quarter = placed("last_quarter", [P, QUARTER, PACK], BF16, LAST_QUARTER_AT)
        interleave_on_scalar(last_quarter[:], v_raw[DRAFT, 1][:, :, QUARTER:HALF])

        v_codes = {}
        v_scales = {}
        for n, (g, h) in enumerate(v_il):
            v_codes[g, h] = new_tile("v_codes%d%d" % (g, h), [P, HALF], U32)
            v_scales[g, h] = placed("v_scales%d%d" % (g, h), [P, HALF], U8, VALUE_SCALES_AT + HALF * n)
            quantize(v_codes[g, h][:], v_scales[g, h][:], v_il[g, h][:])

        wt_il = [new_tile("wt_il%d" % g, [P, Q, PACK], BF16) for g in range(2)]
        wt_codes = [new_tile("wt_codes%d" % g, [P, Q], U32) for g in range(2)]
        wt_scales = [new_tile("wt_scales%d" % g, [P, Q], U8) for g in range(2)]
        for g, copy in ((PREFIX, nc.scalar.copy), (DRAFT, nc.vector.tensor_copy)):
            pairs = wt_il[g][:].rearrange("p q t -> p (q t)").bitcast(F32).rearrange("p (q u) -> p q u", u=2)
            copy(out=pairs, in_=wt_ps[g][:].rearrange("p u q -> p q u"))
        for g in range(2):
            quantize(wt_codes[g][:], wt_scales[g][:], wt_il[g][:])

        v_codes[DRAFT, 1] = new_tile("v_codes11", [P, HALF], U32)
        v_scales[DRAFT, 1] = new_tile("v_scales11", [P, HALF], U8, reuses="wt_il0")
        for n, quarter in enumerate((third_quarter, last_quarter)):
            cols = slice(QUARTER * n, QUARTER * (n + 1))
            quantize(v_codes[DRAFT, 1][:, cols], v_scales[DRAFT, 1][:, cols], quarter[:])

        acc = [ps.tile([P, HALF], F32, name="acc%d" % h, tag="acc%d" % h) for h in range(2)]
        for g in range(2):
            for h in range(2):
                mx_pass(
                    acc[h][:], wt_codes[g][:], wt_scales[g][:], v_codes[g, h][:], v_scales[g, h][:], g == 0, g == 1
                )
        for h, copy in enumerate((nc.scalar.copy, nc.vector.tensor_copy)):
            result = new_tile("result%d" % h, [P, HALF], F32)
            copy(out=result[:], in_=acc[h][:])
            nc.sync.dma_start(out=out[:, HALF * h : HALF * (h + 1)], in_=result[:])
